import numpy as np
CORES = [83,219,339,475,86,222,342,478]
N = 8
def setup_inputs(rng):
    return {"x": rng.standard_normal((N, 128, 512), dtype=np.float32)}
def reference(x):
    s = x.sum(axis=0, dtype=np.float64).astype(x.dtype)
    return {"y": np.broadcast_to(s, (N,) + s.shape)}

@@ -1,0 +1,75 @@
+from concourse.bass import DstId, RemoteDMATransfer
+
+SCRATCH = {
+    "xs": ("dram", [8, 128, 64], "float32"),
+    "res": ("dram", [8, 128, 64], "float32"),
+}
+SEMAPHORES = ["ld_off", "ld_on", "sent", "arr", "res_e", "res_o", "st"]
+
+N_CORES = (0, 2, 4, 7)
+M_CORES = (2, 3, 6, 7)
+
+
+def _wc(host, chip, k):
+    return host * 128 + chip * 8 + k
+
+
+def rank_program(g, core, T, topo):
+    h, c, k = topo.host(core), topo.chip(core), core % 8
+    rank_chip = {}
+    for r in T.cores:
+        rank_chip[topo.host(r)] = topo.chip(r)
+    rank_ks = sorted(set([r % 8 for r in T.cores]))
+    rc = rank_chip[h]
+
+    def dst_id(d):
+        rid, pid = topo.addr(d, core)
+        return DstId(rid=rid, pnc=pid)
+
+    if T.rank_of(core) is not None:
+        w_on = rc & 1
+        w_off = 1 - w_on
+        g.sync.dma_start(T.xs[4 * w_off:4 * w_off + 4], T.x[64 * w_off:64 * w_off + 64, :]).then_inc(T.sem.ld_off, 16)
+        g.scalar.dma_start(T.xs[4 * w_on:4 * w_on + 4], T.x[64 * w_on:64 * w_on + 64, :]).then_inc(T.sem.ld_on, 16)
+        slot = 2 * (h & 1) + rank_ks.index(k)
+        g.wait_ge(T.sem.ld_off, 16)
+        g.remote_dma_fused(
+            [RemoteDMATransfer(dst_ids=[dst_id(_wc(h ^ 1, rc ^ 1, N_CORES[j]))], dma_engine_mask=0x3 << (2 * j),
+                               remote_sem=T.sem.arr, src=T.xs[4 * w_off + j], dst=T.res[slot]) for j in range(4)],
+            local_sem=T.sem.sent)
+        g.wait_ge(T.sem.ld_on, 16)
+        g.remote_dma_fused(
+            [RemoteDMATransfer(dst_ids=[dst_id(_wc(h, rc, N_CORES[j]))], dma_engine_mask=0x300 << (2 * j),
+                               remote_sem=T.sem.arr, src=T.xs[4 * w_on + j], dst=T.res[slot]) for j in range(4)],
+            local_sem=T.sem.sent)
+        g.sync.wait_ge(T.sem.res_e, 32)
+        g.sync.dma_start(T.y[0:64, :], T.res[0:4]).then_inc(T.sem.st, 16)
+        g.scalar.wait_ge(T.sem.res_o, 32)
+        g.scalar.dma_start(T.y[64:128, :], T.res[4:8]).then_inc(T.sem.st, 16)
+        g.wait_ge(T.sem.sent, 16)
+        g.wait_ge(T.sem.st, 32)
+        return
+
+    if c == rc and k in N_CORES:
+        j = N_CORES.index(k)
+        g.wait_ge(T.sem.arr, 8)
+        dsts = [_wc(h ^ 1, c, M_CORES[j]), _wc(3 - h, c, M_CORES[j])]
+        g.remote_dma_fused(
+            [RemoteDMATransfer(dst_ids=[dst_id(d) for d in dsts], dma_engine_mask=0xFF, remote_sem=T.sem.arr,
+                               srcs=[T.res[s] for s in range(4)], dsts=[T.res[topo.rack(h)] for d in dsts], alu_op=1)],
+            local_sem=T.sem.sent)
+        g.wait_ge(T.sem.sent, 8)
+        return
+
+    if c == (rc ^ 1) and k in M_CORES:
+        j = M_CORES.index(k)
+        p = 4 * (c & 1) + j
+        g.wait_ge(T.sem.arr, 16)
+        dsts = [_wc(h, c ^ 1, rk) for rk in rank_ks] + [_wc(h ^ 1, c, rk) for rk in rank_ks]
+        g.remote_dma_fused(
+            [RemoteDMATransfer(dst_ids=[dst_id(d) for d in dsts], dma_engine_mask=0xFF,
+                               remote_sem=T.sem.res_o if c & 1 else T.sem.res_e,
+                               srcs=[T.res[0], T.res[1]], dsts=[T.res[p] for d in dsts], alu_op=1)],
+            local_sem=T.sem.sent)
+        g.wait_ge(T.sem.sent, 8)
+        return

@@ -1,10 +1,15 @@
 from concourse.bass import DstId, RemoteDMATransfer
 
+K = 2
+W = 64 // K
+R = 16 // K
+
 SCRATCH = {
-    "xs": ("dram", [8, 128, 64], "float32"),
-    "res": ("dram", [8, 128, 64], "float32"),
+    "xs": ("dram", [8 * K, 128, W], "float32"),
+    "res": ("dram", [8 * K, 128, W], "float32"),
 }
-SEMAPHORES = ["ld_off", "ld_on", "sent", "arr", "res_e", "res_o", "st"]
+SEMAPHORES = (["sent", "st"] + ["ld%d" % q for q in range(K)] + ["arr%d" % q for q in range(K)]
+              + ["res_e%d" % q for q in range(K)] + ["res_o%d" % q for q in range(K)])
 
 N_CORES = (0, 2, 4, 7)
 M_CORES = (2, 3, 6, 7)
@@ -28,48 +33,53 @@ def rank_program(g, core, T, topo):
 
     if T.rank_of(core) is not None:
         w_on = rc & 1
-        w_off = 1 - w_on
-        g.sync.dma_start(T.xs[4 * w_off:4 * w_off + 4], T.x[64 * w_off:64 * w_off + 64, :]).then_inc(T.sem.ld_off, 16)
-        g.scalar.dma_start(T.xs[4 * w_on:4 * w_on + 4], T.x[64 * w_on:64 * w_on + 64, :]).then_inc(T.sem.ld_on, 16)
-        slot = 2 * (h & 1) + rank_ks.index(k)
-        g.wait_ge(T.sem.ld_off, 16)
-        g.remote_dma_fused(
-            [RemoteDMATransfer(dst_ids=[dst_id(_wc(h ^ 1, rc ^ 1, N_CORES[j]))], dma_engine_mask=0x3 << (2 * j),
-                               remote_sem=T.sem.arr, src=T.xs[4 * w_off + j], dst=T.res[slot]) for j in range(4)],
-            local_sem=T.sem.sent)
-        g.wait_ge(T.sem.ld_on, 16)
-        g.remote_dma_fused(
-            [RemoteDMATransfer(dst_ids=[dst_id(_wc(h, rc, N_CORES[j]))], dma_engine_mask=0x300 << (2 * j),
-                               remote_sem=T.sem.arr, src=T.xs[4 * w_on + j], dst=T.res[slot]) for j in range(4)],
-            local_sem=T.sem.sent)
-        g.sync.wait_ge(T.sem.res_e, 32)
-        g.sync.dma_start(T.y[0:64, :], T.res[0:4]).then_inc(T.sem.st, 16)
-        g.scalar.wait_ge(T.sem.res_o, 32)
-        g.scalar.dma_start(T.y[64:128, :], T.res[4:8]).then_inc(T.sem.st, 16)
-        g.wait_ge(T.sem.sent, 16)
-        g.wait_ge(T.sem.st, 32)
+        for q in range(K):
+            for w, queue in ((0, g.sync), (1, g.scalar)):
+                s = 8 * q + 4 * w
+                queue.dma_start(T.xs[s:s + 4], T.x[s * R:(s + 4) * R, :]).then_inc(T.sem["ld%d" % q], 16)
+        sender = 2 * (h & 1) + rank_ks.index(k)
+        for q in range(K):
+            g.wait_ge(T.sem["ld%d" % q], 32)
+            trs = []
+            for p in range(8):
+                w, j = p // 4, p % 4
+                on = w == w_on
+                d = _wc(h, rc, N_CORES[j]) if on else _wc(h ^ 1, rc ^ 1, N_CORES[j])
+                trs.append(RemoteDMATransfer(dst_ids=[dst_id(d)], dma_engine_mask=(0x300 if on else 0x3) << (2 * j),
+                                             remote_sem=T.sem["arr%d" % q], src=T.xs[8 * q + p], dst=T.res[4 * q + sender]))
+            g.remote_dma_fused(trs, local_sem=T.sem.sent)
+        for q in range(K):
+            for w, queue, name in ((0, g.sync, "res_e%d"), (1, g.scalar, "res_o%d")):
+                s = 8 * q + 4 * w
+                queue.wait_ge(T.sem[name % q], 32)
+                queue.dma_start(T.y[s * R:(s + 4) * R, :], T.res[s:s + 4]).then_inc(T.sem.st, 16)
+        g.wait_ge(T.sem.sent, 16 * K)
+        g.wait_ge(T.sem.st, 32 * K)
         return
 
     if c == rc and k in N_CORES:
         j = N_CORES.index(k)
-        g.wait_ge(T.sem.arr, 8)
         dsts = [_wc(h ^ 1, c, M_CORES[j]), _wc(3 - h, c, M_CORES[j])]
-        g.remote_dma_fused(
-            [RemoteDMATransfer(dst_ids=[dst_id(d) for d in dsts], dma_engine_mask=0xFF, remote_sem=T.sem.arr,
-                               srcs=[T.res[s] for s in range(4)], dsts=[T.res[topo.rack(h)] for d in dsts], alu_op=1)],
-            local_sem=T.sem.sent)
-        g.wait_ge(T.sem.sent, 8)
+        for q in range(K):
+            g.wait_ge(T.sem["arr%d" % q], 8)
+            g.remote_dma_fused(
+                [RemoteDMATransfer(dst_ids=[dst_id(d) for d in dsts], dma_engine_mask=0xFF, remote_sem=T.sem["arr%d" % q],
+                                   srcs=[T.res[4 * q + s] for s in range(4)],
+                                   dsts=[T.res[2 * q + topo.rack(h)] for d in dsts], alu_op=1)],
+                local_sem=T.sem.sent)
+        g.wait_ge(T.sem.sent, 8 * K)
         return
 
     if c == (rc ^ 1) and k in M_CORES:
         j = M_CORES.index(k)
         p = 4 * (c & 1) + j
-        g.wait_ge(T.sem.arr, 16)
         dsts = [_wc(h, c ^ 1, rk) for rk in rank_ks] + [_wc(h ^ 1, c, rk) for rk in rank_ks]
-        g.remote_dma_fused(
-            [RemoteDMATransfer(dst_ids=[dst_id(d) for d in dsts], dma_engine_mask=0xFF,
-                               remote_sem=T.sem.res_o if c & 1 else T.sem.res_e,
-                               srcs=[T.res[0], T.res[1]], dsts=[T.res[p] for d in dsts], alu_op=1)],
-            local_sem=T.sem.sent)
-        g.wait_ge(T.sem.sent, 8)
+        for q in range(K):
+            g.wait_ge(T.sem["arr%d" % q], 16)
+            g.remote_dma_fused(
+                [RemoteDMATransfer(dst_ids=[dst_id(d) for d in dsts], dma_engine_mask=0xFF,
+                                   remote_sem=T.sem[("res_o%d" if c & 1 else "res_e%d") % q],
+                                   srcs=[T.res[2 * q], T.res[2 * q + 1]], dsts=[T.res[8 * q + p] for d in dsts], alu_op=1)],
+                local_sem=T.sem.sent)
+        g.wait_ge(T.sem.sent, 8 * K)
         return

@@ -8,8 +8,8 @@ SCRATCH = {
     "xs": ("dram", [8 * K, 128, W], "float32"),
     "res": ("dram", [8 * K, 128, W], "float32"),
 }
-SEMAPHORES = (["sent", "st"] + ["ld%d" % q for q in range(K)] + ["arr%d" % q for q in range(K)]
-              + ["res_e%d" % q for q in range(K)] + ["res_o%d" % q for q in range(K)])
+SEMAPHORES = (["sent", "st"] + ["ld_off%d" % q for q in range(K)] + ["ld_on%d" % q for q in range(K)]
+              + ["arr%d" % q for q in range(K)] + ["res_e%d" % q for q in range(K)] + ["res_o%d" % q for q in range(K)])
 
 N_CORES = (0, 2, 4, 7)
 M_CORES = (2, 3, 6, 7)
@@ -33,21 +33,21 @@ def rank_program(g, core, T, topo):
 
     if T.rank_of(core) is not None:
         w_on = rc & 1
+        halves = ((1 - w_on, g.sync, "ld_off%d", 0x3), (w_on, g.scalar, "ld_on%d", 0x300))
         for q in range(K):
-            for w, queue in ((0, g.sync), (1, g.scalar)):
+            for w, queue, name, m in halves:
                 s = 8 * q + 4 * w
-                queue.dma_start(T.xs[s:s + 4], T.x[s * R:(s + 4) * R, :]).then_inc(T.sem["ld%d" % q], 16)
+                queue.dma_start(T.xs[s:s + 4], T.x[s * R:(s + 4) * R, :]).then_inc(T.sem[name % q], 16)
         sender = 2 * (h & 1) + rank_ks.index(k)
         for q in range(K):
-            g.wait_ge(T.sem["ld%d" % q], 32)
-            trs = []
-            for p in range(8):
-                w, j = p // 4, p % 4
-                on = w == w_on
-                d = _wc(h, rc, N_CORES[j]) if on else _wc(h ^ 1, rc ^ 1, N_CORES[j])
-                trs.append(RemoteDMATransfer(dst_ids=[dst_id(d)], dma_engine_mask=(0x300 if on else 0x3) << (2 * j),
-                                             remote_sem=T.sem["arr%d" % q], src=T.xs[8 * q + p], dst=T.res[4 * q + sender]))
-            g.remote_dma_fused(trs, local_sem=T.sem.sent)
+            for w, queue, name, m in halves:
+                nh, nc = (h, rc) if w == w_on else (h ^ 1, rc ^ 1)
+                g.wait_ge(T.sem[name % q], 16)
+                g.remote_dma_fused(
+                    [RemoteDMATransfer(dst_ids=[dst_id(_wc(nh, nc, N_CORES[j]))], dma_engine_mask=m << (2 * j),
+                                       remote_sem=T.sem["arr%d" % q], src=T.xs[8 * q + 4 * w + j],
+                                       dst=T.res[4 * q + sender]) for j in range(4)],
+                    local_sem=T.sem.sent)
         for q in range(K):
             for w, queue, name in ((0, g.sync, "res_e%d"), (1, g.scalar, "res_o%d")):
                 s = 8 * q + 4 * w

@@ -31,6 +31,12 @@ def rank_program(g, core, T, topo):
         rid, pid = topo.addr(d, core)
         return DstId(rid=rid, pnc=pid)
 
+    def fold(srcs, dsts, out, sem):
+        g.remote_dma_fused(
+            [RemoteDMATransfer(dst_ids=[dst_id(d) for d in dsts], dma_engine_mask=0xFF, remote_sem=sem,
+                               srcs=srcs, dsts=[out for d in dsts], alu_op=1)],
+            local_sem=T.sem.sent)
+
     if T.rank_of(core) is not None:
         w_on = rc & 1
         halves = ((1 - w_on, g.sync, "ld_off%d", 0x3), (w_on, g.scalar, "ld_on%d", 0x300))
@@ -59,27 +65,20 @@ def rank_program(g, core, T, topo):
 
     if c == rc and k in N_CORES:
         j = N_CORES.index(k)
-        dsts = [_wc(h ^ 1, c, M_CORES[j]), _wc(3 - h, c, M_CORES[j])]
         for q in range(K):
             g.wait_ge(T.sem["arr%d" % q], 8)
-            g.remote_dma_fused(
-                [RemoteDMATransfer(dst_ids=[dst_id(d) for d in dsts], dma_engine_mask=0xFF, remote_sem=T.sem["arr%d" % q],
-                                   srcs=[T.res[4 * q + s] for s in range(4)],
-                                   dsts=[T.res[2 * q + topo.rack(h)] for d in dsts], alu_op=1)],
-                local_sem=T.sem.sent)
-        g.wait_ge(T.sem.sent, 8 * K)
+            for mh in (3 - h, h ^ 1):
+                fold([T.res[4 * q + s] for s in range(4)], [_wc(mh, c, M_CORES[j])], T.res[2 * q + topo.rack(h)],
+                     T.sem["arr%d" % q])
+        g.wait_ge(T.sem.sent, 16 * K)
         return
 
     if c == (rc ^ 1) and k in M_CORES:
         j = M_CORES.index(k)
         p = 4 * (c & 1) + j
-        dsts = [_wc(h, c ^ 1, rk) for rk in rank_ks] + [_wc(h ^ 1, c, rk) for rk in rank_ks]
         for q in range(K):
             g.wait_ge(T.sem["arr%d" % q], 16)
-            g.remote_dma_fused(
-                [RemoteDMATransfer(dst_ids=[dst_id(d) for d in dsts], dma_engine_mask=0xFF,
-                                   remote_sem=T.sem[("res_o%d" if c & 1 else "res_e%d") % q],
-                                   srcs=[T.res[2 * q], T.res[2 * q + 1]], dsts=[T.res[8 * q + p] for d in dsts], alu_op=1)],
-                local_sem=T.sem.sent)
-        g.wait_ge(T.sem.sent, 8 * K)
+            for dsts in ([_wc(h ^ 1, c, rk) for rk in rank_ks], [_wc(h, c ^ 1, rk) for rk in rank_ks]):
+                fold([T.res[2 * q], T.res[2 * q + 1]], dsts, T.res[8 * q + p], T.sem[("res_o%d" if c & 1 else "res_e%d") % q])
+        g.wait_ge(T.sem.sent, 16 * K)
         return

from concourse.bass import DstId, RemoteDMATransfer

K = 2
W = 64 // K
R = 16 // K

SCRATCH = {
    "xs": ("dram", [8 * K, 128, W], "float32"),
    "res": ("dram", [8 * K, 128, W], "float32"),
}
SEMAPHORES = (["sent", "st"] + ["ld_off%d" % q for q in range(K)] + ["ld_on%d" % q for q in range(K)]
              + ["arr%d" % q for q in range(K)] + ["res_e%d" % q for q in range(K)] + ["res_o%d" % q for q in range(K)])

N_CORES = (0, 2, 4, 7)
M_CORES = (2, 3, 6, 7)


def _wc(host, chip, k):
    return host * 128 + chip * 8 + k


def rank_program(g, core, T, topo):
    h, c, k = topo.host(core), topo.chip(core), core % 8
    rank_chip = {}
    for r in T.cores:
        rank_chip[topo.host(r)] = topo.chip(r)
    rank_ks = sorted(set([r % 8 for r in T.cores]))
    rc = rank_chip[h]

    def dst_id(d):
        rid, pid = topo.addr(d, core)
        return DstId(rid=rid, pnc=pid)

    def fold(srcs, dsts, out, sem):
        g.remote_dma_fused(
            [RemoteDMATransfer(dst_ids=[dst_id(d) for d in dsts], dma_engine_mask=0xFF, remote_sem=sem,
                               srcs=srcs, dsts=[out for d in dsts], alu_op=1)],
            local_sem=T.sem.sent)

    if T.rank_of(core) is not None:
        w_on = rc & 1
        halves = ((1 - w_on, g.sync, "ld_off%d", 0x3), (w_on, g.scalar, "ld_on%d", 0x300))
        for q in range(K):
            for w, queue, name, m in halves:
                s = 8 * q + 4 * w
                queue.dma_start(T.xs[s:s + 4], T.x[s * R:(s + 4) * R, :]).then_inc(T.sem[name % q], 16)
        sender = 2 * (h & 1) + rank_ks.index(k)
        for q in range(K):
            for w, queue, name, m in halves:
                nh, nc = (h, rc) if w == w_on else (h ^ 1, rc ^ 1)
                g.wait_ge(T.sem[name % q], 16)
                g.remote_dma_fused(
                    [RemoteDMATransfer(dst_ids=[dst_id(_wc(nh, nc, N_CORES[j]))], dma_engine_mask=m << (2 * j),
                                       remote_sem=T.sem["arr%d" % q], src=T.xs[8 * q + 4 * w + j],
                                       dst=T.res[4 * q + sender]) for j in range(4)],
                    local_sem=T.sem.sent)
        for q in range(K):
            for w, queue, name in ((0, g.sync, "res_e%d"), (1, g.scalar, "res_o%d")):
                s = 8 * q + 4 * w
                queue.wait_ge(T.sem[name % q], 32)
                queue.dma_start(T.y[s * R:(s + 4) * R, :], T.res[s:s + 4]).then_inc(T.sem.st, 16)
        g.wait_ge(T.sem.sent, 16 * K)
        g.wait_ge(T.sem.st, 32 * K)
        return

    if c == rc and k in N_CORES:
        j = N_CORES.index(k)
        for q in range(K):
            g.wait_ge(T.sem["arr%d" % q], 8)
            for mh in (3 - h, h ^ 1):
                fold([T.res[4 * q + s] for s in range(4)], [_wc(mh, c, M_CORES[j])], T.res[2 * q + topo.rack(h)],
                     T.sem["arr%d" % q])
        g.wait_ge(T.sem.sent, 16 * K)
        return

    if c == (rc ^ 1) and k in M_CORES:
        j = M_CORES.index(k)
        p = 4 * (c & 1) + j
        for q in range(K):
            g.wait_ge(T.sem["arr%d" % q], 16)
            for dsts in ([_wc(h ^ 1, c, rk) for rk in rank_ks], [_wc(h, c ^ 1, rk) for rk in rank_ks]):
                fold([T.res[2 * q], T.res[2 * q + 1]], dsts, T.res[8 * q + p], T.sem[("res_o%d" if c & 1 else "res_e%d") % q])
        g.wait_ge(T.sem.sent, 16 * K)
        return
